import numpy as np
import ml_dtypes


def mxq(x, axis, fmt="e4m3"):
    dtype, down = {"e4m3": (ml_dtypes.float8_e4m3fn, 7), "e5m2": (ml_dtypes.float8_e5m2, 14)}[fmt]
    v = np.moveaxis(np.asarray(x, np.float32).astype(ml_dtypes.bfloat16).astype(np.float64), axis, -1)
    blocks = v.reshape(v.shape[:-1] + (-1, 32))
    amax = np.abs(blocks).max(-1, keepdims=True)
    byte = np.maximum(np.where(amax > 0, np.frexp(amax)[1] - 1 + 127, 0) - down, 1)
    scale = np.exp2(byte - 127.0)
    codes = (blocks / scale).astype(np.float32).astype(dtype).astype(np.float64)
    return np.moveaxis((codes * scale).reshape(v.shape), -1, axis)


WIDE = False


def mx_kscale(k):
    if not WIDE:
        return np.ones(k)
    levels = np.array([10, -10, 5, -5, 0])
    if k % 512:
        return np.exp2(np.random.permutation(np.resize(levels, k // 32))).repeat(32)
    a = np.empty((k // 512, 16))
    for p in range(k // 512):
        a[p, :8] = np.random.permutation(np.resize(levels, 8))
        for g in range(8):
            far = levels[np.abs(levels - a[p, g]) >= 10]
            a[p, g + 8] = far[np.random.randint(len(far))]
    return np.exp2(a.ravel()).repeat(32)


def f64(x):
    return np.asarray(x).astype(np.float64)


def striped(idx):
    return np.tile(idx.reshape(-1, 16).T, (8, 1)).astype(np.uint16)


def unstriped(offs):
    return offs[:16].T.reshape(-1).astype(np.int64)


E2M1 = np.array([0.0, 0.5, 1.0, 1.5, 2.0, 3.0, 4.0, 6.0, -0.0, -0.5, -1.0, -1.5, -2.0, -3.0, -4.0, -6.0])


def pack_weight(w, fmt):
    k, n = w.shape
    w = f64(np.asarray(w, np.float32).astype(ml_dtypes.bfloat16)).reshape(k // 32, 32, n)
    amax = np.abs(w).max(1)
    if fmt == "e4m3":
        byte = np.frexp(amax)[1] - 1 + 127 - 7
    else:
        mant, ex = np.frexp(amax / 6.0)
        byte = np.where(mant > 0.5, ex, ex - 1) + 127
    byte = np.clip(np.where(amax > 0, byte, 1), 1, 254)
    scaled = (w * np.exp2(127.0 - byte)[:, None, :]).reshape(k, n).astype(np.float32)
    by_word = np.ascontiguousarray(scaled.reshape(k // 512, 128, 4, n).transpose(0, 1, 3, 2))
    if fmt == "e4m3":
        words = by_word.astype(ml_dtypes.float8_e4m3fn).view(np.uint8)
    else:
        c = by_word.astype(ml_dtypes.float4_e2m1fn).view(np.uint8) & 0xF
        words = (c[..., 0::2] | (c[..., 1::2] << 4)).reshape(k // 512, 128, 2 * n)
    return np.ascontiguousarray(words), np.ascontiguousarray(byte.astype(np.uint8).reshape(k // 512, 16, n))


def unpack_weight(words, scales, fmt):
    g, _, n = scales.shape
    words = np.ascontiguousarray(words).reshape(g, 128, n, -1)
    if fmt == "e4m3":
        vals = words.view(ml_dtypes.float8_e4m3fn).astype(np.float64)
    else:
        nib = np.empty((g, 128, n, 4), np.uint8)
        nib[..., 0::2] = words & 0xF
        nib[..., 1::2] = words >> 4
        vals = E2M1[nib]
    vals = vals * np.repeat(np.exp2(scales.astype(np.float64) - 127.0), 8, axis=1)[..., None]
    return vals.transpose(0, 1, 3, 2).reshape(g * 512, n)


def gelu(v):
    return 0.5 * v * (1.0 + np.tanh(np.sqrt(2.0 / np.pi) * (v + 0.044715 * v**3)))


def twice(P):
    return np.random.permutation(np.repeat(np.arange(P), 2))


K, H, T, S, P = 1024, 1024, 4096, 1024, 512

def setup_inputs():
    n = np.random.standard_normal
    s = mx_kscale(K)[:, None]
    u = mx_kscale(H)[:, None]
    d = {}
    d["tab_words"], d["tab_scales"] = pack_weight(n((K, T)) * s, "e4m3")
    d["offs"] = striped(np.random.permutation(T)[:S])
    d["pos1"] = striped(np.random.permutation(S)[:P])
    d["pos2"] = striped(np.random.permutation(S)[:P])
    d["pos3"] = striped(twice(P))
    d["wa"] = (n((K, H)) / K ** 0.5 / s * u.T).astype(np.float32)
    d["wb_words"], d["wb_scales"] = pack_weight(n((K, H)) / K ** 0.5 / s * u.T, "e4m3")
    d["w2_words"], d["w2_scales"] = pack_weight(n((H, H)) / H ** 0.5 / u, "e2m1")
    d["gain"] = (np.exp(0.3 * n(H)) / u[:, 0]).astype(np.float32)
    return d

def reference(tab_words, tab_scales, offs, pos1, pos2, pos3, wa, wb_words, wb_scales, w2_words, w2_scales, gain):
    v = unpack_weight(tab_words, tab_scales, "e4m3")[:, unstriped(offs)]
    wb = unpack_weight(wb_words, wb_scales, "e4m3")
    w2 = unpack_weight(w2_words, w2_scales, "e2m1")
    a = mxq(f64(wa), 0, "e4m3").T @ v
    b = wb.T @ v
    h = a - np.abs(b)
    x = np.maximum(h[:, unstriped(pos1)], h[:, unstriped(pos2)])
    y = w2.T @ mxq(x, 0, "e4m3")
    back = y[:, unstriped(pos3)]
    return f64(gain)[:, None] * h / (1.0 + back * back)

@@ -1,0 +1,247 @@
+from contextlib import ExitStack
+
+import concourse.mybir as mybir
+
+K, H, T, S, M = 1024, 1024, 4096, 1024, 512
+FLOPS = 2 * K * H * S * 2 + 2 * H * H * M
+
+F32 = mybir.dt.float32
+BF16 = mybir.dt.bfloat16
+I32 = mybir.dt.int32
+U32 = mybir.dt.uint32
+U16 = mybir.dt.uint16
+U8 = mybir.dt.uint8
+FP8X4 = mybir.dt.float8_e4m3fn_x4
+FP4X4 = mybir.dt.float4_e2m1fn_x4
+ACT = mybir.ActivationFunctionType
+ALU = mybir.AluOpType
+
+P = 128
+PACK = 4
+PASS = P * PACK
+NPASS = K // PASS
+NBLK = H // PASS
+BANK = 512
+SPARE = 32
+
+
+def tile_list_kettle_seed_monitor_kernel(
+    tc, tab_words, tab_scales, offs, pos1, pos2, pos3, wa, wb_words, wb_scales, w2_words, w2_scales, gain, out
+):
+    nc = tc.nc
+    with ExitStack() as ctx:
+        keep = ctx.enter_context(tc.tile_pool(name="keep", bufs=1))
+        ring = ctx.enter_context(tc.tile_pool(name="ring", bufs=3))
+        psum = ctx.enter_context(tc.psum_pool(name="psum", bufs=8))
+
+        def held(shape, dtype, name):
+            return keep.tile(shape, dtype, name=name, align_bytes=64)
+
+        offs_sb = keep.tile([P, S // 16], U16, name="offs_sb")
+        pos1_sb = keep.tile([P, M // 16], U16, name="pos1_sb")
+        pos2_sb = keep.tile([P, M // 16], U16, name="pos2_sb")
+        pos3_sb = keep.tile([P, S // 16], U16, name="pos3_sb")
+        tab_w = [held([P, T], I32, "tab_w%d" % a) for a in range(NPASS)]
+        tab_s = held([P, T], U8, "tab_s")
+        v_w = [held([P, S], U32, "v_w%d" % a) for a in range(NPASS)]
+        v_s = held([P, S], U8, "v_s")
+        wa_raw = [[held([P, PACK, PASS], F32, "wa_raw%d%d" % (b, a)) for a in range(NPASS)] for b in range(NBLK)]
+        wa_w = [[held([P, PASS], U32, "wa_w%d%d" % (b, a)) for a in range(NPASS)] for b in range(NBLK)]
+        wa_s = [[held([P, PASS], U8, "wa_s%d%d" % (b, a)) for a in range(NPASS)] for b in range(NBLK)]
+        wb_raw = [held([P, NPASS * PASS], I32, "wb_raw%d" % b) for b in range(NBLK)]
+        wb_w = [held([P, NPASS * PASS], I32, "wb_w%d" % b) for b in range(NBLK)]
+        wbs_raw = held([P, H], U8, "wbs_raw")
+        wb_s = held([P, H], U8, "wb_s")
+        w2_raw = held([P, NBLK * H * 2], U8, "w2_raw")
+        w2_w = held([P, NBLK * H * 2], U8, "w2_w")
+        w2s_raw = held([P, NBLK * H], U8, "w2s_raw")
+        w2_s = held([P, NBLK * H], U8, "w2_s")
+        gain_sb = held([P, NBLK, PACK], F32, "gain_sb")
+        h = [held([P, S], F32, "h%d" % n) for n in range(NBLK * PACK)]
+        pick1 = held([P, PACK, M], F32, "pick1")
+        pick2 = held([P, PACK, M], F32, "pick2")
+        x_bf = held([P, M * PACK], BF16, "x_bf")
+        x_w = [held([P, M], U32, "x_w%d" % b) for b in range(NBLK)]
+        x_s = [held([P, M], U8, "x_s%d" % b) for b in range(NBLK)]
+        y = [held([P, M + SPARE], F32, "y%d" % n) for n in range(NBLK * PACK)]
+        warm = held([P, 2], F32, "warm")
+
+        nc.vector.memset(tab_s[:].bitcast(I32), 0)
+        nc.vector.memset(wbs_raw[:].bitcast(I32), 0)
+        nc.vector.memset(w2s_raw[:].bitcast(I32), 0)
+        nc.vector.memset(warm[:, 0:1], 1.0)
+        nc.scalar.activation(warm[:, 1:2], warm[:, 0:1], ACT.Abs_reciprocal_sqrt)
+        for n in range(NBLK * PACK):
+            nc.vector.memset(y[n][:, M:], 0.0)
+
+        def load_wa(b, a):
+            rows = wa[PASS * a : PASS * (a + 1), PASS * b : PASS * (b + 1)]
+            nc.sync.dma_start(wa_raw[b][a][:], rows.rearrange("(p j) c -> p j c", j=PACK))
+
+        def load_wb(b):
+            cols = wb_words[:, :, PASS * b : PASS * (b + 1), :].rearrange("a p c i -> p a (c i)")
+            nc.sync.dma_start(wb_raw[b][:].rearrange("p (a c) -> p a c", a=NPASS), cols.bitcast(I32))
+
+        nc.sync.dma_start(offs_sb[:], offs)
+        for a in range(NPASS):
+            nc.sync.dma_start(tab_w[a][:], tab_words[a].rearrange("p t i -> p (t i)").bitcast(I32))
+        load_wb(0)
+        load_wa(0, 0)
+        load_wa(0, 1)
+        nc.sync.dma_start(pos1_sb[:], pos1)
+        nc.sync.dma_start(pos2_sb[:], pos2)
+        nc.sync.dma_start(
+            w2_raw[:].bitcast(I32).rearrange("p (a c) -> p a c", a=NBLK),
+            w2_words.rearrange("a p c -> p a c").bitcast(I32),
+        )
+        load_wb(1)
+        load_wa(1, 0)
+        load_wa(1, 1)
+        nc.sync.dma_start(pos3_sb[:], pos3)
+        nc.sync.dma_start(gain_sb[:], gain.rearrange("(b p t) -> p b t", p=P, t=PACK))
+
+        for q in range(4):
+            nc.gpsimd.dma_start(
+                tab_s[32 * q : 32 * q + 8, :].bitcast(I32), tab_scales[:, 4 * q : 4 * q + 4, :].bitcast(I32)
+            )
+        for q in range(4):
+            nc.gpsimd.dma_start(
+                wbs_raw[32 * q : 32 * q + 8, :].bitcast(I32), wb_scales[:, 4 * q : 4 * q + 4, :].bitcast(I32)
+            )
+        for q in range(4):
+            nc.gpsimd.dma_start(
+                w2s_raw[32 * q : 32 * q + 4, :].bitcast(I32).rearrange("p (a c) -> p a c", a=NBLK),
+                w2_scales[:, 4 * q : 4 * q + 4, :].rearrange("a r c -> r a c").bitcast(I32),
+            )
+
+        def deal(dst, src):
+            nc.vector.tensor_copy(
+                dst.rearrange("p (g t m) -> p g m t", t=PACK, m=P), src.rearrange("p (g m t) -> p g m t", t=PACK, m=P)
+            )
+
+        def round_wa(b, a, copy):
+            wa_bf = ring.tile([P, PASS * PACK], BF16, name="wa_bf", align_bytes=64, bufs=2)
+            copy(
+                wa_bf[:].rearrange("p (t m j) -> p m j t", t=PACK, j=PACK),
+                wa_raw[b][a][:].rearrange("p j (m t) -> p m j t", t=PACK),
+            )
+            return wa_bf
+
+        def quantise_wa(b, a, wa_bf):
+            nc.vector.quantize_mx(out=wa_w[b][a][:].bitcast(FP8X4), scales=wa_s[b][a][:], in_=wa_bf[:])
+
+        nc.vector.tensor_copy(v_s[:], tab_s[:].indirect(offs_sb[:]))
+        nc.vector.tensor_copy(v_w[0][:], tab_w[0][:].bitcast(U32).indirect(offs_sb[:]))
+        deal(wb_s[:], wbs_raw[:])
+        nc.vector.tensor_copy(v_w[1][:], tab_w[1][:].bitcast(U32).indirect(offs_sb[:]))
+        deal(wb_w[0][:], wb_raw[0][:])
+        quantise_wa(0, 0, round_wa(0, 0, nc.scalar.copy))
+        quantise_wa(0, 1, round_wa(0, 1, nc.vector.tensor_copy))
+
+        def features(n, half):
+            b, t = divmod(n, PACK)
+            cols = slice(BANK * half, BANK * (half + 1))
+            rows = slice(P * t, P * (t + 1))
+            acc_b = psum.tile([P, BANK], F32, name="acc")
+            for a in range(NPASS):
+                nc.tensor.matmul_mx(
+                    out=acc_b[:],
+                    lhsT=wb_w[b][:, PASS * a + P * t : PASS * a + P * (t + 1)].bitcast(FP8X4),
+                    lhsT_scale=wb_s[4 * a :, PASS * b + P * t : PASS * b + P * (t + 1)],
+                    rhs=v_w[a][:, cols].bitcast(FP8X4),
+                    rhs_scale=v_s[4 * a :, cols],
+                    start=(a == 0),
+                    stop=(a == NPASS - 1),
+                )
+            acc_a = psum.tile([P, BANK], F32, name="acc")
+            for a in range(NPASS):
+                nc.tensor.matmul_mx(
+                    out=acc_a[:],
+                    lhsT=wa_w[b][a][:, rows].bitcast(FP8X4),
+                    lhsT_scale=wa_s[b][a][:, rows],
+                    rhs=v_w[a][:, cols].bitcast(FP8X4),
+                    rhs_scale=v_s[4 * a :, cols],
+                    start=(a == 0),
+                    stop=(a == NPASS - 1),
+                )
+            size = ring.tile([P, BANK], F32, name="size")
+            nc.scalar.activation(size[:], acc_b[:], ACT.Abs)
+            nc.vector.tensor_tensor(h[n][:, cols], acc_a[:], size[:], ALU.subtract)
+
+        def pick(n, picks, pos_sb):
+            nc.vector.tensor_copy(picks[:, n % PACK, :], h[n][:].indirect(pos_sb[:]))
+
+        def kettles(b):
+            nc.vector.tensor_tensor(
+                x_bf[:].rearrange("p (c i t) -> p c t i", i=4, t=PACK),
+                pick1[:].rearrange("p t (c i) -> p c t i", i=4),
+                pick2[:].rearrange("p t (c i) -> p c t i", i=4),
+                ALU.max,
+            )
+            nc.vector.quantize_mx(out=x_w[b][:].bitcast(FP8X4), scales=x_s[b][:], in_=x_bf[:])
+
+        ntile = NBLK * PACK
+        for n in range(ntile + 1):
+            if n < ntile:
+                features(n, 0)
+            if n > 0:
+                pick(n - 1, pick1, pos1_sb)
+            if n < ntile:
+                features(n, 1)
+            if n > 0:
+                pick(n - 1, pick2, pos2_sb)
+                if n % PACK == 0:
+                    kettles(n // PACK - 1)
+            if n == 0:
+                deal(w2_w[:].bitcast(U16), w2_raw[:].bitcast(U16))
+                deal(w2_s[:], w2s_raw[:])
+            if n == 1:
+                deal(wb_w[1][:], wb_raw[1][:])
+                quantise_wa(1, 0, round_wa(1, 0, nc.scalar.copy))
+            if n == 2:
+                quantise_wa(1, 1, round_wa(1, 1, nc.scalar.copy))
+
+        out_rows = out.rearrange("(b p t) j -> b t p j", p=P, t=PACK)
+
+        def kettle_result(n):
+            acc_y = psum.tile([P, BANK], F32, name="acc")
+            for a in range(NBLK):
+                first = H * a + P * n
+                nc.tensor.matmul_mx(
+                    out=acc_y[:],
+                    lhsT=w2_w[:, 2 * first : 2 * (first + P)].bitcast(FP4X4),
+                    lhsT_scale=w2_s[:, first : first + P],
+                    rhs=x_w[a][:].bitcast(FP8X4),
+                    rhs_scale=x_s[a][:],
+                    start=(a == 0),
+                    stop=(a == NBLK - 1),
+                )
+            nc.scalar.copy(y[n][:, :M], acc_y[:])
+
+        def damping(u):
+            n, half = divmod(u, 2)
+            back = ring.tile([P, BANK], F32, name="back")
+            nc.vector.tensor_copy(back[:], y[n][:].indirect(pos3_sb[:, 32 * half : 32 * (half + 1)]))
+            damp = ring.tile([P, BANK], F32, name="damp")
+            nc.scalar.activation(damp[:], back[:], ACT.Square)
+            nc.scalar.activation(back[:], damp[:], ACT.Abs_reciprocal_sqrt, bias=1.0)
+            nc.scalar.activation(damp[:], back[:], ACT.Square)
+            return damp
+
+        def finish(u, damp):
+            n, half = divmod(u, 2)
+            b, t = divmod(n, PACK)
+            cols = slice(BANK * half, BANK * (half + 1))
+            res = ring.tile([P, BANK], F32, name="res", bufs=4)
+            nc.vector.scalar_tensor_tensor(res[:], h[n][:, cols], gain_sb[:, b, t : t + 1], damp[:], ALU.mult, ALU.mult)
+            nc.sync.dma_start(out_rows[b, t, :, cols], res[:])
+
+        damps = {}
+        kettle_result(0)
+        for u in range(2 * ntile + 2):
+            if u < ntile - 1:
+                kettle_result(u + 1)
+            if u < 2 * ntile:
+                damps[u] = damping(u)
+            if u >= 2:
+                finish(u - 2, damps[u - 2])

@@ -60,13 +60,12 @@ def tile_list_kettle_seed_monitor_kernel(
         h = [held([P, S], F32, "h%d" % n) for n in range(NBLK * PACK)]
         pick1 = held([P, PACK, M], F32, "pick1")
         pick2 = held([P, PACK, M], F32, "pick2")
-        x_bf = held([P, M * PACK], BF16, "x_bf")
         x_w = [held([P, M], U32, "x_w%d" % b) for b in range(NBLK)]
         x_s = [held([P, M], U8, "x_s%d" % b) for b in range(NBLK)]
         y = [held([P, M + SPARE], F32, "y%d" % n) for n in range(NBLK * PACK)]
         warm = held([P, 2], F32, "warm")
 
-        nc.vector.memset(tab_s[:].bitcast(I32), 0)
+        nc.gpsimd.memset(tab_s[:].bitcast(I32), 0)
         nc.vector.memset(wbs_raw[:].bitcast(I32), 0)
         nc.vector.memset(w2s_raw[:].bitcast(I32), 0)
         nc.vector.memset(warm[:, 0:1], 1.0)
@@ -83,47 +82,47 @@ def tile_list_kettle_seed_monitor_kernel(
             nc.sync.dma_start(wb_raw[b][:].rearrange("p (a c) -> p a c", a=NPASS), cols.bitcast(I32))
 
         nc.sync.dma_start(offs_sb[:], offs)
+        nc.sync.dma_start(pos1_sb[:], pos1)
+        nc.sync.dma_start(pos2_sb[:], pos2)
+        nc.sync.dma_start(pos3_sb[:], pos3)
+        nc.sync.dma_start(gain_sb[:], gain.rearrange("(b p t) -> p b t", p=P, t=PACK))
         for a in range(NPASS):
             nc.sync.dma_start(tab_w[a][:], tab_words[a].rearrange("p t i -> p (t i)").bitcast(I32))
         load_wb(0)
-        load_wa(0, 0)
-        load_wa(0, 1)
-        nc.sync.dma_start(pos1_sb[:], pos1)
-        nc.sync.dma_start(pos2_sb[:], pos2)
-        nc.sync.dma_start(
-            w2_raw[:].bitcast(I32).rearrange("p (a c) -> p a c", a=NBLK),
-            w2_words.rearrange("a p c -> p a c").bitcast(I32),
-        )
-        load_wb(1)
-        load_wa(1, 0)
-        load_wa(1, 1)
-        nc.sync.dma_start(pos3_sb[:], pos3)
-        nc.sync.dma_start(gain_sb[:], gain.rearrange("(b p t) -> p b t", p=P, t=PACK))
-
         for q in range(4):
             nc.gpsimd.dma_start(
                 tab_s[32 * q : 32 * q + 8, :].bitcast(I32), tab_scales[:, 4 * q : 4 * q + 4, :].bitcast(I32)
             )
         for q in range(4):
-            nc.gpsimd.dma_start(
+            nc.sync.dma_start(
                 wbs_raw[32 * q : 32 * q + 8, :].bitcast(I32), wb_scales[:, 4 * q : 4 * q + 4, :].bitcast(I32)
             )
+        load_wa(0, 0)
+        load_wa(0, 1)
+        nc.sync.dma_start(
+            w2_raw[:].bitcast(I32).rearrange("p (a c) -> p a c", a=NBLK),
+            w2_words.rearrange("a p c -> p a c").bitcast(I32),
+        )
         for q in range(4):
-            nc.gpsimd.dma_start(
+            nc.sync.dma_start(
                 w2s_raw[32 * q : 32 * q + 4, :].bitcast(I32).rearrange("p (a c) -> p a c", a=NBLK),
                 w2_scales[:, 4 * q : 4 * q + 4, :].rearrange("a r c -> r a c").bitcast(I32),
             )
+        load_wb(1)
+        load_wa(1, 0)
+        load_wa(1, 1)
 
-        def deal(dst, src):
+        def deal(dst, src, run):
             nc.vector.tensor_copy(
-                dst.rearrange("p (g t m) -> p g m t", t=PACK, m=P), src.rearrange("p (g m t) -> p g m t", t=PACK, m=P)
+                dst.rearrange("p (g t c i) -> p g c t i", t=PACK, c=P // run, i=run),
+                src.rearrange("p (g c i t) -> p g c t i", t=PACK, c=P // run, i=run),
             )
 
         def round_wa(b, a, copy):
             wa_bf = ring.tile([P, PASS * PACK], BF16, name="wa_bf", align_bytes=64, bufs=2)
             copy(
-                wa_bf[:].rearrange("p (t m j) -> p m j t", t=PACK, j=PACK),
-                wa_raw[b][a][:].rearrange("p j (m t) -> p m j t", t=PACK),
+                wa_bf[:].rearrange("p (t m j) -> p m t j", t=PACK, j=PACK),
+                wa_raw[b][a][:].rearrange("p j (m t) -> p m t j", t=PACK),
             )
             return wa_bf
 
@@ -132,9 +131,9 @@ def tile_list_kettle_seed_monitor_kernel(
 
         nc.vector.tensor_copy(v_s[:], tab_s[:].indirect(offs_sb[:]))
         nc.vector.tensor_copy(v_w[0][:], tab_w[0][:].bitcast(U32).indirect(offs_sb[:]))
-        deal(wb_s[:], wbs_raw[:])
+        deal(wb_s[:], wbs_raw[:], 16)
         nc.vector.tensor_copy(v_w[1][:], tab_w[1][:].bitcast(U32).indirect(offs_sb[:]))
-        deal(wb_w[0][:], wb_raw[0][:])
+        deal(wb_w[0][:], wb_raw[0][:], 4)
         quantise_wa(0, 0, round_wa(0, 0, nc.scalar.copy))
         quantise_wa(0, 1, round_wa(0, 1, nc.vector.tensor_copy))
 
@@ -172,13 +171,19 @@ def tile_list_kettle_seed_monitor_kernel(
             nc.vector.tensor_copy(picks[:, n % PACK, :], h[n][:].indirect(pos_sb[:]))
 
         def kettles(b):
-            nc.vector.tensor_tensor(
-                x_bf[:].rearrange("p (c i t) -> p c t i", i=4, t=PACK),
-                pick1[:].rearrange("p t (c i) -> p c t i", i=4),
-                pick2[:].rearrange("p t (c i) -> p c t i", i=4),
-                ALU.max,
-            )
-            nc.vector.quantize_mx(out=x_w[b][:].bitcast(FP8X4), scales=x_s[b][:], in_=x_bf[:])
+            halves = [slice(M // 2 * k, M // 2 * (k + 1)) for k in range(2)]
+            x_bf = [ring.tile([P, M // 2 * PACK], BF16, name="x_bf", align_bytes=64, bufs=2) for k in range(2)]
+            for k in range(2):
+                nc.vector.tensor_tensor(
+                    x_bf[k][:].rearrange("p (c i t) -> p c t i", i=2, t=PACK),
+                    pick1[:, :, halves[k]].rearrange("p t (c i) -> p c t i", i=2),
+                    pick2[:, :, halves[k]].rearrange("p t (c i) -> p c t i", i=2),
+                    ALU.max,
+                )
+            for k in range(2):
+                nc.vector.quantize_mx(
+                    out=x_w[b][:, halves[k]].bitcast(FP8X4), scales=x_s[b][:, halves[k]], in_=x_bf[k][:]
+                )
 
         ntile = NBLK * PACK
         for n in range(ntile + 1):
@@ -193,38 +198,46 @@ def tile_list_kettle_seed_monitor_kernel(
                 if n % PACK == 0:
                     kettles(n // PACK - 1)
             if n == 0:
-                deal(w2_w[:].bitcast(U16), w2_raw[:].bitcast(U16))
-                deal(w2_s[:], w2s_raw[:])
+                deal(w2_w[:].bitcast(U16), w2_raw[:].bitcast(U16), 8)
+                deal(w2_s[:], w2s_raw[:], 16)
             if n == 1:
-                deal(wb_w[1][:], wb_raw[1][:])
+                deal(wb_w[1][:], wb_raw[1][:], 4)
                 quantise_wa(1, 0, round_wa(1, 0, nc.scalar.copy))
             if n == 2:
                 quantise_wa(1, 1, round_wa(1, 1, nc.scalar.copy))
 
         out_rows = out.rearrange("(b p t) j -> b t p j", p=P, t=PACK)
 
-        def kettle_result(n):
-            acc_y = psum.tile([P, BANK], F32, name="acc")
-            for a in range(NBLK):
-                first = H * a + P * n
-                nc.tensor.matmul_mx(
-                    out=acc_y[:],
-                    lhsT=w2_w[:, 2 * first : 2 * (first + P)].bitcast(FP4X4),
-                    lhsT_scale=w2_s[:, first : first + P],
-                    rhs=x_w[a][:].bitcast(FP8X4),
-                    rhs_scale=x_s[a][:],
-                    start=(a == 0),
-                    stop=(a == NBLK - 1),
-                )
-            nc.scalar.copy(y[n][:, :M], acc_y[:])
+        acc_y = [psum.tile([P, BANK], F32, name="acc") for n in range(ntile)]
 
-        def damping(u):
+        def kettle_pass(n, a):
+            first = H * a + P * n
+            nc.tensor.matmul_mx(
+                out=acc_y[n][:],
+                lhsT=w2_w[:, 2 * first : 2 * (first + P)].bitcast(FP4X4),
+                lhsT_scale=w2_s[:, first : first + P],
+                rhs=x_w[a][:].bitcast(FP8X4),
+                rhs_scale=x_s[a][:],
+                start=(a == 0),
+                stop=(a == NBLK - 1),
+            )
+
+        for a in range(NBLK):
+            for n in range(ntile):
+                kettle_pass(n, a)
+
+        def kettle_result(n):
+            copy = nc.vector.tensor_copy if n in (0, 3, 5, 7) else nc.scalar.copy
+            copy(y[n][:, :M], acc_y[n][:])
+
+        def fetch(u):
             n, half = divmod(u, 2)
-            back = ring.tile([P, BANK], F32, name="back")
+            back = ring.tile([P, BANK], F32, name="back", bufs=5)
             nc.vector.tensor_copy(back[:], y[n][:].indirect(pos3_sb[:, 32 * half : 32 * (half + 1)]))
-            damp = ring.tile([P, BANK], F32, name="damp")
-            nc.scalar.activation(damp[:], back[:], ACT.Square)
-            nc.scalar.activation(back[:], damp[:], ACT.Abs_reciprocal_sqrt, bias=1.0)
+            return back
+
+        def square(back):
+            damp = ring.tile([P, BANK], F32, name="damp", bufs=5)
             nc.scalar.activation(damp[:], back[:], ACT.Square)
             return damp
 
@@ -232,16 +245,25 @@ def tile_list_kettle_seed_monitor_kernel(
             n, half = divmod(u, 2)
             b, t = divmod(n, PACK)
             cols = slice(BANK * half, BANK * (half + 1))
-            res = ring.tile([P, BANK], F32, name="res", bufs=4)
+            res = ring.tile([P, BANK], F32, name="res")
             nc.vector.scalar_tensor_tensor(res[:], h[n][:, cols], gain_sb[:, b, t : t + 1], damp[:], ALU.mult, ALU.mult)
             nc.sync.dma_start(out_rows[b, t, :, cols], res[:])
 
-        damps = {}
+        backs, damps = {}, {}
+        nunit = 2 * ntile
         kettle_result(0)
-        for u in range(2 * ntile + 2):
-            if u < ntile - 1:
-                kettle_result(u + 1)
-            if u < 2 * ntile:
-                damps[u] = damping(u)
-            if u >= 2:
-                finish(u - 2, damps[u - 2])
+        kettle_result(1)
+        kettle_result(2)
+        for u in range(nunit + 4):
+            if u % 2 == 1 and u // 2 + 3 < ntile:
+                kettle_result(u // 2 + 3)
+            if u < nunit:
+                backs[u] = fetch(u)
+            if 0 <= u - 1 < nunit:
+                damps[u - 1] = square(backs[u - 1])
+            if 0 <= u - 2 < nunit:
+                nc.scalar.activation(backs[u - 2][:], damps[u - 2][:], ACT.Abs_reciprocal_sqrt, bias=1.0)
+            if 0 <= u - 3 < nunit:
+                nc.scalar.activation(damps[u - 3][:], backs[u - 3][:], ACT.Square)
+            if 0 <= u - 4 < nunit:
+                finish(u - 4, damps[u - 4])

@@ -45,7 +45,7 @@ def tile_list_kettle_seed_monitor_kernel(
         tab_s = held([P, T], U8, "tab_s")
         v_w = [held([P, S], U32, "v_w%d" % a) for a in range(NPASS)]
         v_s = held([P, S], U8, "v_s")
-        wa_raw = [[held([P, PACK, PASS], F32, "wa_raw%d%d" % (b, a)) for a in range(NPASS)] for b in range(NBLK)]
+        wa_raw = [[ring.tile([P, PACK, PASS], F32, name="wa_raw", bufs=4) for a in range(NPASS)] for b in range(NBLK)]
         wa_w = [[held([P, PASS], U32, "wa_w%d%d" % (b, a)) for a in range(NPASS)] for b in range(NBLK)]
         wa_s = [[held([P, PASS], U8, "wa_s%d%d" % (b, a)) for a in range(NPASS)] for b in range(NBLK)]
         wb_raw = [held([P, NPASS * PASS], I32, "wb_raw%d" % b) for b in range(NBLK)]
@@ -54,8 +54,8 @@ def tile_list_kettle_seed_monitor_kernel(
         wb_s = held([P, H], U8, "wb_s")
         w2_raw = held([P, NBLK * H * 2], U8, "w2_raw")
         w2_w = held([P, NBLK * H * 2], U8, "w2_w")
-        w2s_raw = held([P, NBLK * H], U8, "w2s_raw")
-        w2_s = held([P, NBLK * H], U8, "w2_s")
+        w2s_raw = held([P, H], U8, "w2s_raw")
+        w2_s = [held([P, H], U8, "w2_s%d" % a) for a in range(NBLK)]
         gain_sb = held([P, NBLK, PACK], F32, "gain_sb")
         h = [held([P, S], F32, "h%d" % n) for n in range(NBLK * PACK)]
         pick1 = held([P, PACK, M], F32, "pick1")
@@ -65,9 +65,10 @@ def tile_list_kettle_seed_monitor_kernel(
         y = [held([P, M + SPARE], F32, "y%d" % n) for n in range(NBLK * PACK)]
         warm = held([P, 2], F32, "warm")
 
-        nc.gpsimd.memset(tab_s[:].bitcast(I32), 0)
+        nc.vector.memset(tab_s[:].bitcast(I32), 0)
         nc.vector.memset(wbs_raw[:].bitcast(I32), 0)
         nc.vector.memset(w2s_raw[:].bitcast(I32), 0)
+        nc.vector.memset(w2_s[1][:].bitcast(I32), 0)
         nc.vector.memset(warm[:, 0:1], 1.0)
         nc.scalar.activation(warm[:, 1:2], warm[:, 0:1], ACT.Abs_reciprocal_sqrt)
         for n in range(NBLK * PACK):
@@ -81,36 +82,38 @@ def tile_list_kettle_seed_monitor_kernel(
             cols = wb_words[:, :, PASS * b : PASS * (b + 1), :].rearrange("a p c i -> p a (c i)")
             nc.sync.dma_start(wb_raw[b][:].rearrange("p (a c) -> p a c", a=NPASS), cols.bitcast(I32))
 
-        nc.sync.dma_start(offs_sb[:], offs)
-        nc.sync.dma_start(pos1_sb[:], pos1)
-        nc.sync.dma_start(pos2_sb[:], pos2)
-        nc.sync.dma_start(pos3_sb[:], pos3)
-        nc.sync.dma_start(gain_sb[:], gain.rearrange("(b p t) -> p b t", p=P, t=PACK))
-        for a in range(NPASS):
+        def load_tab(a):
             nc.sync.dma_start(tab_w[a][:], tab_words[a].rearrange("p t i -> p (t i)").bitcast(I32))
-        load_wb(0)
+
+        load_tab(0)
         for q in range(4):
-            nc.gpsimd.dma_start(
+            nc.sync.dma_start(
                 tab_s[32 * q : 32 * q + 8, :].bitcast(I32), tab_scales[:, 4 * q : 4 * q + 4, :].bitcast(I32)
             )
+        nc.sync.dma_start(offs_sb[:], offs)
+        load_tab(1)
+        load_wb(0)
         for q in range(4):
             nc.sync.dma_start(
                 wbs_raw[32 * q : 32 * q + 8, :].bitcast(I32), wb_scales[:, 4 * q : 4 * q + 4, :].bitcast(I32)
             )
-        load_wa(0, 0)
-        load_wa(0, 1)
         nc.sync.dma_start(
             w2_raw[:].bitcast(I32).rearrange("p (a c) -> p a c", a=NBLK),
             w2_words.rearrange("a p c -> p a c").bitcast(I32),
         )
+        load_wa(0, 0)
+        load_wa(0, 1)
+        nc.sync.dma_start(pos1_sb[:], pos1)
+        nc.sync.dma_start(pos2_sb[:], pos2)
         for q in range(4):
             nc.sync.dma_start(
-                w2s_raw[32 * q : 32 * q + 4, :].bitcast(I32).rearrange("p (a c) -> p a c", a=NBLK),
-                w2_scales[:, 4 * q : 4 * q + 4, :].rearrange("a r c -> r a c").bitcast(I32),
+                w2s_raw[32 * q : 32 * q + 8, :].bitcast(I32), w2_scales[:, 4 * q : 4 * q + 4, :].bitcast(I32)
             )
-        load_wb(1)
         load_wa(1, 0)
         load_wa(1, 1)
+        load_wb(1)
+        nc.sync.dma_start(pos3_sb[:], pos3)
+        nc.sync.dma_start(gain_sb[:], gain.rearrange("(b p t) -> p b t", p=P, t=PACK))
 
         def deal(dst, src, run):
             nc.vector.tensor_copy(
@@ -118,24 +121,28 @@ def tile_list_kettle_seed_monitor_kernel(
                 src.rearrange("p (g c i t) -> p g c t i", t=PACK, c=P // run, i=run),
             )
 
-        def round_wa(b, a, copy):
-            wa_bf = ring.tile([P, PASS * PACK], BF16, name="wa_bf", align_bytes=64, bufs=2)
+        def round_wa(b, a, t0, nt, copy):
+            wa_bf = ring.tile([P, P * nt * PACK], BF16, name="wa_bf", align_bytes=64, bufs=3)
             copy(
-                wa_bf[:].rearrange("p (t m j) -> p m t j", t=PACK, j=PACK),
-                wa_raw[b][a][:].rearrange("p j (m t) -> p m t j", t=PACK),
+                wa_bf[:].rearrange("p (t m j) -> p m t j", t=nt, j=PACK),
+                wa_raw[b][a][:].rearrange("p j (m t) -> p m t j", t=PACK)[:, :, t0 : t0 + nt, :],
             )
             return wa_bf
 
-        def quantise_wa(b, a, wa_bf):
-            nc.vector.quantize_mx(out=wa_w[b][a][:].bitcast(FP8X4), scales=wa_s[b][a][:], in_=wa_bf[:])
+        def quantise_wa(b, a, t0, nt, copy):
+            cols = slice(P * t0, P * (t0 + nt))
+            wa_bf = round_wa(b, a, t0, nt, copy)
+            nc.vector.quantize_mx(out=wa_w[b][a][:, cols].bitcast(FP8X4), scales=wa_s[b][a][:, cols], in_=wa_bf[:])
 
-        nc.vector.tensor_copy(v_s[:], tab_s[:].indirect(offs_sb[:]))
         nc.vector.tensor_copy(v_w[0][:], tab_w[0][:].bitcast(U32).indirect(offs_sb[:]))
-        deal(wb_s[:], wbs_raw[:], 16)
+        nc.vector.tensor_copy(v_s[:], tab_s[:].indirect(offs_sb[:]))
         nc.vector.tensor_copy(v_w[1][:], tab_w[1][:].bitcast(U32).indirect(offs_sb[:]))
+        deal(wb_s[:], wbs_raw[:], 16)
         deal(wb_w[0][:], wb_raw[0][:], 4)
-        quantise_wa(0, 0, round_wa(0, 0, nc.scalar.copy))
-        quantise_wa(0, 1, round_wa(0, 1, nc.vector.tensor_copy))
+        deal(w2_w[:].bitcast(U16), w2_raw[:].bitcast(U16), 8)
+        quantise_wa(0, 0, 0, 4, nc.scalar.copy)
+        quantise_wa(0, 1, 0, 2, nc.vector.tensor_copy)
+        quantise_wa(0, 1, 2, 2, nc.scalar.copy)
 
         def features(n, half):
             b, t = divmod(n, PACK)
@@ -163,7 +170,7 @@ def tile_list_kettle_seed_monitor_kernel(
                     start=(a == 0),
                     stop=(a == NPASS - 1),
                 )
-            size = ring.tile([P, BANK], F32, name="size")
+            size = ring.tile([P, BANK], F32, name="size", bufs=4)
             nc.scalar.activation(size[:], acc_b[:], ACT.Abs)
             nc.vector.tensor_tensor(h[n][:, cols], acc_a[:], size[:], ALU.subtract)
 
@@ -198,13 +205,16 @@ def tile_list_kettle_seed_monitor_kernel(
                 if n % PACK == 0:
                     kettles(n // PACK - 1)
             if n == 0:
-                deal(w2_w[:].bitcast(U16), w2_raw[:].bitcast(U16), 8)
-                deal(w2_s[:], w2s_raw[:], 16)
+                deal(w2_s[0][:], w2s_raw[:], 16)
+                for q in range(4):
+                    nc.sync.dma_start(
+                        w2_s[1][32 * q : 32 * q + 4, :].bitcast(I32), w2_s[0][32 * q + 4 : 32 * q + 8, :].bitcast(I32)
+                    )
             if n == 1:
-                deal(wb_w[1][:], wb_raw[1][:], 4)
-                quantise_wa(1, 0, round_wa(1, 0, nc.scalar.copy))
+                quantise_wa(1, 0, 0, 4, nc.scalar.copy)
             if n == 2:
-                quantise_wa(1, 1, round_wa(1, 1, nc.scalar.copy))
+                quantise_wa(1, 1, 0, 4, nc.scalar.copy)
+                deal(wb_w[1][:], wb_raw[1][:], 4)
 
         out_rows = out.rearrange("(b p t) j -> b t p j", p=P, t=PACK)
 
@@ -215,7 +225,7 @@ def tile_list_kettle_seed_monitor_kernel(
             nc.tensor.matmul_mx(
                 out=acc_y[n][:],
                 lhsT=w2_w[:, 2 * first : 2 * (first + P)].bitcast(FP4X4),
-                lhsT_scale=w2_s[:, first : first + P],
+                lhsT_scale=w2_s[a][:, P * n : P * (n + 1)],
                 rhs=x_w[a][:].bitcast(FP8X4),
                 rhs_scale=x_s[a][:],
                 start=(a == 0),
@@ -227,17 +237,17 @@ def tile_list_kettle_seed_monitor_kernel(
                 kettle_pass(n, a)
 
         def kettle_result(n):
-            copy = nc.vector.tensor_copy if n in (0, 3, 5, 7) else nc.scalar.copy
+            copy = nc.vector.tensor_copy if n in (0, 4, 6) else nc.scalar.copy
             copy(y[n][:, :M], acc_y[n][:])
 
         def fetch(u):
             n, half = divmod(u, 2)
-            back = ring.tile([P, BANK], F32, name="back", bufs=5)
+            back = ring.tile([P, BANK], F32, name="back", bufs=6)
             nc.vector.tensor_copy(back[:], y[n][:].indirect(pos3_sb[:, 32 * half : 32 * (half + 1)]))
             return back
 
         def square(back):
-            damp = ring.tile([P, BANK], F32, name="damp", bufs=5)
+            damp = ring.tile([P, BANK], F32, name="damp", bufs=6)
             nc.scalar.activation(damp[:], back[:], ACT.Square)
             return damp
 
@@ -245,9 +255,9 @@ def tile_list_kettle_seed_monitor_kernel(
             n, half = divmod(u, 2)
             b, t = divmod(n, PACK)
             cols = slice(BANK * half, BANK * (half + 1))
-            res = ring.tile([P, BANK], F32, name="res")
-            nc.vector.scalar_tensor_tensor(res[:], h[n][:, cols], gain_sb[:, b, t : t + 1], damp[:], ALU.mult, ALU.mult)
-            nc.sync.dma_start(out_rows[b, t, :, cols], res[:])
+            res = h[n][:, cols]
+            nc.vector.scalar_tensor_tensor(res, res, gain_sb[:, b, t : t + 1], damp[:], ALU.mult, ALU.mult)
+            nc.sync.dma_start(out_rows[b, t, :, cols], res)
 
         backs, damps = {}, {}
         nunit = 2 * ntile

@@ -1,9 +1,10 @@
 from contextlib import ExitStack
 
 import concourse.mybir as mybir
+from concourse.masks import make_identity
 
 K, H, T, S, M = 1024, 1024, 4096, 1024, 512
-FLOPS = 2 * K * H * S * 2 + 2 * H * H * M
+FLOPS = 2 * (2 * K * H * S) + 2 * H * H * M
 
 F32 = mybir.dt.float32
 BF16 = mybir.dt.bfloat16
@@ -21,8 +22,15 @@ PACK = 4
 PASS = P * PACK
 NPASS = K // PASS
 NBLK = H // PASS
+NTILE = NBLK * PACK
 BANK = 512
+NHALF = S // BANK
+QUADRANT = 32
+ROWS = 4
+GROUP = 16
+LINE = 16
 SPARE = 32
+DEPTH = 6
 
 
 def tile_list_kettle_seed_monitor_kernel(
@@ -37,243 +45,281 @@ def tile_list_kettle_seed_monitor_kernel(
         def held(shape, dtype, name):
             return keep.tile(shape, dtype, name=name, align_bytes=64)
 
-        offs_sb = keep.tile([P, S // 16], U16, name="offs_sb")
-        pos1_sb = keep.tile([P, M // 16], U16, name="pos1_sb")
-        pos2_sb = keep.tile([P, M // 16], U16, name="pos2_sb")
-        pos3_sb = keep.tile([P, S // 16], U16, name="pos3_sb")
+        def bank():
+            return psum.tile([P, BANK], F32, name="bank")
+
+        def work(tag):
+            return ring.tile([P, BANK], F32, name=tag, bufs=DEPTH)
+
+        offs_sb = keep.tile([P, S // GROUP], U16, name="offs_sb")
+        pos1_sb = keep.tile([P, M // GROUP], U16, name="pos1_sb")
+        pos2_sb = keep.tile([P, M // GROUP], U16, name="pos2_sb")
+        pos3_sb = keep.tile([P, S // GROUP], U16, name="pos3_sb")
         tab_w = [held([P, T], I32, "tab_w%d" % a) for a in range(NPASS)]
         tab_s = held([P, T], U8, "tab_s")
         v_w = [held([P, S], U32, "v_w%d" % a) for a in range(NPASS)]
         v_s = held([P, S], U8, "v_s")
-        wa_raw = [[ring.tile([P, PACK, PASS], F32, name="wa_raw", bufs=4) for a in range(NPASS)] for b in range(NBLK)]
+        wa_raw = [[held([P, PACK, PASS], F32, "wa_raw%d%d" % (b, a)) for a in range(NPASS)] for b in range(NBLK)]
         wa_w = [[held([P, PASS], U32, "wa_w%d%d" % (b, a)) for a in range(NPASS)] for b in range(NBLK)]
         wa_s = [[held([P, PASS], U8, "wa_s%d%d" % (b, a)) for a in range(NPASS)] for b in range(NBLK)]
-        wb_raw = [held([P, NPASS * PASS], I32, "wb_raw%d" % b) for b in range(NBLK)]
+        wb_w_raw = [held([P, NPASS * PASS], I32, "wb_w_raw%d" % b) for b in range(NBLK)]
         wb_w = [held([P, NPASS * PASS], I32, "wb_w%d" % b) for b in range(NBLK)]
-        wbs_raw = held([P, H], U8, "wbs_raw")
+        wb_s_raw = held([P, H], U8, "wb_s_raw")
         wb_s = held([P, H], U8, "wb_s")
-        w2_raw = held([P, NBLK * H * 2], U8, "w2_raw")
+        w2_w_raw = held([P, NBLK * H * 2], U8, "w2_w_raw")
         w2_w = held([P, NBLK * H * 2], U8, "w2_w")
-        w2s_raw = held([P, H], U8, "w2s_raw")
-        w2_s = [held([P, H], U8, "w2_s%d" % a) for a in range(NBLK)]
+        w2_s_raw = held([P, H], U8, "w2_s_raw")
+        w2_s = [held([P, H], U8, "w2_s%d" % b) for b in range(NBLK)]
         gain_sb = held([P, NBLK, PACK], F32, "gain_sb")
-        h = [held([P, S], F32, "h%d" % n) for n in range(NBLK * PACK)]
-        pick1 = held([P, PACK, M], F32, "pick1")
-        pick2 = held([P, PACK, M], F32, "pick2")
+        h = [held([P, S], F32, "h%d" % n) for n in range(NTILE)]
+        picked1 = held([P, PACK, M], F32, "picked1")
+        picked2 = held([P, PACK, M], F32, "picked2")
         x_w = [held([P, M], U32, "x_w%d" % b) for b in range(NBLK)]
         x_s = [held([P, M], U8, "x_s%d" % b) for b in range(NBLK)]
-        y = [held([P, M + SPARE], F32, "y%d" % n) for n in range(NBLK * PACK)]
-        warm = held([P, 2], F32, "warm")
+        y = [held([P, M + SPARE], F32, "y%d" % n) for n in range(NTILE)]
+        seed = held([P, 1], F32, "seed")
+        root = held([P, 1], F32, "root")
+        one = held([P, 1], F32, "one")
+        ident = held([P, P], F32, "ident")
+        make_identity(nc, ident[:])
 
-        nc.vector.memset(tab_s[:].bitcast(I32), 0)
-        nc.vector.memset(wbs_raw[:].bitcast(I32), 0)
-        nc.vector.memset(w2s_raw[:].bitcast(I32), 0)
-        nc.vector.memset(w2_s[1][:].bitcast(I32), 0)
-        nc.vector.memset(warm[:, 0:1], 1.0)
-        nc.scalar.activation(warm[:, 1:2], warm[:, 0:1], ACT.Abs_reciprocal_sqrt)
-        for n in range(NBLK * PACK):
+        for plane in (tab_s, wb_s_raw, w2_s_raw, w2_s[1]):
+            nc.vector.memset(plane[:].bitcast(I32), 0)
+        nc.vector.memset(seed[:], 1.0)
+        nc.scalar.activation(root[:], seed[:], ACT.Abs_reciprocal_sqrt)
+        nc.scalar.activation(one[:], root[:], ACT.Sign)
+        for n in range(NTILE):
             nc.vector.memset(y[n][:, M:], 0.0)
 
-        def load_wa(b, a):
-            rows = wa[PASS * a : PASS * (a + 1), PASS * b : PASS * (b + 1)]
-            nc.sync.dma_start(wa_raw[b][a][:], rows.rearrange("(p j) c -> p j c", j=PACK))
-
-        def load_wb(b):
-            cols = wb_words[:, :, PASS * b : PASS * (b + 1), :].rearrange("a p c i -> p a (c i)")
-            nc.sync.dma_start(wb_raw[b][:].rearrange("p (a c) -> p a c", a=NPASS), cols.bitcast(I32))
-
-        def load_tab(a):
+        def load_tab_words(a):
             nc.sync.dma_start(tab_w[a][:], tab_words[a].rearrange("p t i -> p (t i)").bitcast(I32))
 
-        load_tab(0)
-        for q in range(4):
-            nc.sync.dma_start(
-                tab_s[32 * q : 32 * q + 8, :].bitcast(I32), tab_scales[:, 4 * q : 4 * q + 4, :].bitcast(I32)
-            )
+        def load_planes(tile, scales):
+            for q in range(P // QUADRANT):
+                nc.sync.dma_start(
+                    tile[QUADRANT * q : QUADRANT * q + 2 * ROWS, :].bitcast(I32),
+                    scales[:, ROWS * q : ROWS * (q + 1), :].bitcast(I32),
+                )
+
+        def load_wa(b, a):
+            part = wa[PASS * a : PASS * (a + 1), PASS * b : PASS * (b + 1)]
+            nc.sync.dma_start(wa_raw[b][a][:], part.rearrange("(p j) c -> p j c", j=PACK))
+
+        def load_wb_words(b):
+            part = wb_words[:, :, PASS * b : PASS * (b + 1), :].rearrange("a p c i -> p a (c i)")
+            nc.sync.dma_start(wb_w_raw[b][:].rearrange("p (a c) -> p a c", a=NPASS), part.bitcast(I32))
+
+        load_tab_words(0)
+        load_planes(tab_s, tab_scales)
         nc.sync.dma_start(offs_sb[:], offs)
-        load_tab(1)
-        load_wb(0)
-        for q in range(4):
-            nc.sync.dma_start(
-                wbs_raw[32 * q : 32 * q + 8, :].bitcast(I32), wb_scales[:, 4 * q : 4 * q + 4, :].bitcast(I32)
-            )
+        load_tab_words(1)
+        load_wb_words(0)
+        load_planes(wb_s_raw, wb_scales)
         nc.sync.dma_start(
-            w2_raw[:].bitcast(I32).rearrange("p (a c) -> p a c", a=NBLK),
-            w2_words.rearrange("a p c -> p a c").bitcast(I32),
+            w2_w_raw[:].bitcast(I32).rearrange("p (b c) -> p b c", b=NBLK),
+            w2_words.rearrange("b p c -> p b c").bitcast(I32),
         )
         load_wa(0, 0)
         load_wa(0, 1)
         nc.sync.dma_start(pos1_sb[:], pos1)
         nc.sync.dma_start(pos2_sb[:], pos2)
-        for q in range(4):
-            nc.sync.dma_start(
-                w2s_raw[32 * q : 32 * q + 8, :].bitcast(I32), w2_scales[:, 4 * q : 4 * q + 4, :].bitcast(I32)
-            )
+        load_planes(w2_s_raw, w2_scales)
         load_wa(1, 0)
         load_wa(1, 1)
-        load_wb(1)
+        load_wb_words(1)
         nc.sync.dma_start(pos3_sb[:], pos3)
         nc.sync.dma_start(gain_sb[:], gain.rearrange("(b p t) -> p b t", p=P, t=PACK))
 
-        def deal(dst, src, run):
+        def deal(dst, src, element_bytes):
+            run = LINE // element_bytes
             nc.vector.tensor_copy(
                 dst.rearrange("p (g t c i) -> p g c t i", t=PACK, c=P // run, i=run),
                 src.rearrange("p (g c i t) -> p g c t i", t=PACK, c=P // run, i=run),
             )
 
-        def round_wa(b, a, t0, nt, copy):
-            wa_bf = ring.tile([P, P * nt * PACK], BF16, name="wa_bf", align_bytes=64, bufs=3)
+        def quantise_wa(b, a, t_first, t_count, copy):
+            wa_bf = ring.tile([P, P * t_count * PACK], BF16, name="wa_bf", align_bytes=64)
             copy(
-                wa_bf[:].rearrange("p (t m j) -> p m t j", t=nt, j=PACK),
-                wa_raw[b][a][:].rearrange("p j (m t) -> p m t j", t=PACK)[:, :, t0 : t0 + nt, :],
+                wa_bf[:].rearrange("p (t m j) -> p m t j", t=t_count, j=PACK),
+                wa_raw[b][a][:].rearrange("p j (m t) -> p m t j", t=PACK)[:, :, t_first : t_first + t_count, :],
             )
-            return wa_bf
-
-        def quantise_wa(b, a, t0, nt, copy):
-            cols = slice(P * t0, P * (t0 + nt))
-            wa_bf = round_wa(b, a, t0, nt, copy)
+            cols = slice(P * t_first, P * (t_first + t_count))
             nc.vector.quantize_mx(out=wa_w[b][a][:, cols].bitcast(FP8X4), scales=wa_s[b][a][:, cols], in_=wa_bf[:])
 
         nc.vector.tensor_copy(v_w[0][:], tab_w[0][:].bitcast(U32).indirect(offs_sb[:]))
         nc.vector.tensor_copy(v_s[:], tab_s[:].indirect(offs_sb[:]))
         nc.vector.tensor_copy(v_w[1][:], tab_w[1][:].bitcast(U32).indirect(offs_sb[:]))
-        deal(wb_s[:], wbs_raw[:], 16)
-        deal(wb_w[0][:], wb_raw[0][:], 4)
-        deal(w2_w[:].bitcast(U16), w2_raw[:].bitcast(U16), 8)
-        quantise_wa(0, 0, 0, 4, nc.scalar.copy)
-        quantise_wa(0, 1, 0, 2, nc.vector.tensor_copy)
-        quantise_wa(0, 1, 2, 2, nc.scalar.copy)
+        deal(wb_s[:], wb_s_raw[:], 1)
+        deal(wb_w[0][:], wb_w_raw[0][:], 4)
+        deal(w2_w[:].bitcast(U16), w2_w_raw[:].bitcast(U16), 2)
+        quantise_wa(0, 0, 0, PACK, nc.scalar.copy)
+        quantise_wa(0, 1, 0, PACK // 2, nc.vector.tensor_copy)
+        quantise_wa(0, 1, PACK // 2, PACK // 2, nc.scalar.copy)
 
-        def features(n, half):
+        def v_operand(a, probes):
+            return v_w[a][:, probes].bitcast(FP8X4), v_s[ROWS * a :, probes]
+
+        def wa_operand(a, n):
             b, t = divmod(n, PACK)
-            cols = slice(BANK * half, BANK * (half + 1))
-            rows = slice(P * t, P * (t + 1))
-            acc_b = psum.tile([P, BANK], F32, name="acc")
-            for a in range(NPASS):
-                nc.tensor.matmul_mx(
-                    out=acc_b[:],
-                    lhsT=wb_w[b][:, PASS * a + P * t : PASS * a + P * (t + 1)].bitcast(FP8X4),
-                    lhsT_scale=wb_s[4 * a :, PASS * b + P * t : PASS * b + P * (t + 1)],
-                    rhs=v_w[a][:, cols].bitcast(FP8X4),
-                    rhs_scale=v_s[4 * a :, cols],
-                    start=(a == 0),
-                    stop=(a == NPASS - 1),
-                )
-            acc_a = psum.tile([P, BANK], F32, name="acc")
-            for a in range(NPASS):
-                nc.tensor.matmul_mx(
-                    out=acc_a[:],
-                    lhsT=wa_w[b][a][:, rows].bitcast(FP8X4),
-                    lhsT_scale=wa_s[b][a][:, rows],
-                    rhs=v_w[a][:, cols].bitcast(FP8X4),
-                    rhs_scale=v_s[4 * a :, cols],
-                    start=(a == 0),
-                    stop=(a == NPASS - 1),
-                )
-            size = ring.tile([P, BANK], F32, name="size", bufs=4)
-            nc.scalar.activation(size[:], acc_b[:], ACT.Abs)
-            nc.vector.tensor_tensor(h[n][:, cols], acc_a[:], size[:], ALU.subtract)
+            cols = slice(P * t, P * (t + 1))
+            return wa_w[b][a][:, cols].bitcast(FP8X4), wa_s[b][a][:, cols]
 
-        def pick(n, picks, pos_sb):
-            nc.vector.tensor_copy(picks[:, n % PACK, :], h[n][:].indirect(pos_sb[:]))
+        def wb_operand(a, n):
+            b, t = divmod(n, PACK)
+            words = wb_w[b][:, PASS * a + P * t : PASS * a + P * (t + 1)]
+            return words.bitcast(FP8X4), wb_s[ROWS * a :, P * n : P * (n + 1)]
 
-        def kettles(b):
-            halves = [slice(M // 2 * k, M // 2 * (k + 1)) for k in range(2)]
-            x_bf = [ring.tile([P, M // 2 * PACK], BF16, name="x_bf", align_bytes=64, bufs=2) for k in range(2)]
-            for k in range(2):
-                nc.vector.tensor_tensor(
-                    x_bf[k][:].rearrange("p (c i t) -> p c t i", i=2, t=PACK),
-                    pick1[:, :, halves[k]].rearrange("p t (c i) -> p c t i", i=2),
-                    pick2[:, :, halves[k]].rearrange("p t (c i) -> p c t i", i=2),
-                    ALU.max,
-                )
-            for k in range(2):
-                nc.vector.quantize_mx(
-                    out=x_w[b][:, halves[k]].bitcast(FP8X4), scales=x_s[b][:, halves[k]], in_=x_bf[k][:]
-                )
-
-        ntile = NBLK * PACK
-        for n in range(ntile + 1):
-            if n < ntile:
-                features(n, 0)
-            if n > 0:
-                pick(n - 1, pick1, pos1_sb)
-            if n < ntile:
-                features(n, 1)
-            if n > 0:
-                pick(n - 1, pick2, pos2_sb)
-                if n % PACK == 0:
-                    kettles(n // PACK - 1)
-            if n == 0:
-                deal(w2_s[0][:], w2s_raw[:], 16)
-                for q in range(4):
-                    nc.sync.dma_start(
-                        w2_s[1][32 * q : 32 * q + 4, :].bitcast(I32), w2_s[0][32 * q + 4 : 32 * q + 8, :].bitcast(I32)
-                    )
-            if n == 1:
-                quantise_wa(1, 0, 0, 4, nc.scalar.copy)
-            if n == 2:
-                quantise_wa(1, 1, 0, 4, nc.scalar.copy)
-                deal(wb_w[1][:], wb_raw[1][:], 4)
-
-        out_rows = out.rearrange("(b p t) j -> b t p j", p=P, t=PACK)
-
-        acc_y = [psum.tile([P, BANK], F32, name="acc") for n in range(ntile)]
-
-        def kettle_pass(n, a):
-            first = H * a + P * n
+        def mx_pass(acc, stationary, moving, a, passes):
             nc.tensor.matmul_mx(
-                out=acc_y[n][:],
-                lhsT=w2_w[:, 2 * first : 2 * (first + P)].bitcast(FP4X4),
-                lhsT_scale=w2_s[a][:, P * n : P * (n + 1)],
-                rhs=x_w[a][:].bitcast(FP8X4),
-                rhs_scale=x_s[a][:],
+                out=acc,
+                lhsT=stationary[0],
+                lhsT_scale=stationary[1],
+                rhs=moving[0],
+                rhs_scale=moving[1],
                 start=(a == 0),
-                stop=(a == NBLK - 1),
+                stop=(a == passes - 1),
             )
 
-        for a in range(NBLK):
-            for n in range(ntile):
-                kettle_pass(n, a)
+        def direct_half(n, half):
+            probes = slice(BANK * half, BANK * (half + 1))
+            acc_b = bank()
+            for a in range(NPASS):
+                mx_pass(acc_b[:], wb_operand(a, n), v_operand(a, probes), a, NPASS)
+            acc_a = bank()
+            for a in range(NPASS):
+                mx_pass(acc_a[:], wa_operand(a, n), v_operand(a, probes), a, NPASS)
+            size = work("work_a")
+            nc.scalar.activation(size[:], acc_b[:], ACT.Abs)
+            nc.vector.tensor_tensor(h[n][:, probes], acc_a[:], size[:], ALU.subtract)
 
-        def kettle_result(n):
-            copy = nc.vector.tensor_copy if n in (0, 4, 6) else nc.scalar.copy
+        def turned_terms(n, half):
+            acc_b = bank()
+            acc_a = bank()
+            for acc, weight in ((acc_b, wb_operand), (acc_a, wa_operand)):
+                for piece in range(BANK // P):
+                    probes = slice(BANK * half + P * piece, BANK * half + P * (piece + 1))
+                    for a in range(NPASS):
+                        mx_pass(acc[:, P * piece : P * (piece + 1)], v_operand(a, probes), weight(a, n), a, NPASS)
+            size = work("work_a")
+            nc.scalar.activation(size[:], acc_b[:], ACT.Abs)
+            minus_a = work("work_b")
+            nc.scalar.activation(minus_a[:], acc_a[:], ACT.Copy, scale=-1.0)
+            return size, minus_a
+
+        def turn_back(n, half, size, minus_a):
+            acc_h = bank()
+            for piece in range(BANK // P):
+                cols = slice(P * piece, P * (piece + 1))
+                nc.tensor.matmul(acc_h[:, cols], size[:, cols], ident[:], start=True, stop=False, is_transpose=True)
+                nc.tensor.matmul(acc_h[:, cols], minus_a[:, cols], ident[:], start=False, stop=True, is_transpose=True)
+            nc.scalar.activation(h[n][:, BANK * half : BANK * (half + 1)], acc_h[:], ACT.Copy, scale=-1.0)
+
+        def is_turned(n, half):
+            return (half == 1 and n > 0) or (n >= 3 and n % 2 == 1)
+
+        terms = {}
+
+        def make_half(step):
+            if step < NHALF * NTILE:
+                n, half = divmod(step, NHALF)
+                if is_turned(n, half):
+                    terms[step] = turned_terms(n, half)
+                else:
+                    direct_half(n, half)
+            if step - 1 in terms:
+                turn_back(*divmod(step - 1, NHALF), *terms[step - 1])
+
+        def pick(n, picked, pos_sb):
+            nc.vector.tensor_copy(picked[:, n % PACK, :], h[n][:].indirect(pos_sb[:]))
+
+        def quantise_x(b):
+            kettles = [slice(M // 2 * side, M // 2 * (side + 1)) for side in range(2)]
+            x_bf = [ring.tile([P, M // 2 * PACK], BF16, name="x_bf", align_bytes=64, bufs=2) for side in range(2)]
+            for side in range(2):
+                nc.vector.tensor_tensor(
+                    x_bf[side][:].rearrange("p (c i t) -> p c t i", i=2, t=PACK),
+                    picked1[:, :, kettles[side]].rearrange("p t (c i) -> p c t i", i=2),
+                    picked2[:, :, kettles[side]].rearrange("p t (c i) -> p c t i", i=2),
+                    ALU.max,
+                )
+            for side in range(2):
+                nc.vector.quantize_mx(
+                    out=x_w[b][:, kettles[side]].bitcast(FP8X4), scales=x_s[b][:, kettles[side]], in_=x_bf[side][:]
+                )
+
+        def deal_w2_planes():
+            deal(w2_s[0][:], w2_s_raw[:], 1)
+            for q in range(P // QUADRANT):
+                first = QUADRANT * q
+                nc.sync.dma_start(
+                    w2_s[1][first : first + ROWS, :].bitcast(I32),
+                    w2_s[0][first + ROWS : first + 2 * ROWS, :].bitcast(I32),
+                )
+
+        for n in range(NTILE + 1):
+            make_half(NHALF * n)
+            if n > 0:
+                pick(n - 1, picked1, pos1_sb)
+            if n < NTILE:
+                make_half(NHALF * n + 1)
+            if n > 0:
+                pick(n - 1, picked2, pos2_sb)
+                if n % PACK == 0:
+                    quantise_x(n // PACK - 1)
+            if n == 0:
+                deal_w2_planes()
+            if n == 1:
+                quantise_wa(1, 0, 0, PACK, nc.scalar.copy)
+            if n == 2:
+                quantise_wa(1, 1, 0, PACK, nc.scalar.copy)
+                deal(wb_w[1][:], wb_w_raw[1][:], 4)
+
+        acc_y = [bank() for n in range(NTILE)]
+        for b in range(NBLK):
+            for n in range(NTILE):
+                first = H * b + P * n
+                w2_operand = w2_w[:, 2 * first : 2 * (first + P)].bitcast(FP4X4), w2_s[b][:, P * n : P * (n + 1)]
+                mx_pass(acc_y[n][:], w2_operand, (x_w[b][:].bitcast(FP8X4), x_s[b][:]), b, NBLK)
+
+        def copy_y(n):
+            on_vector = n == 0 or (n >= PACK and n % 2 == 0)
+            copy = nc.vector.tensor_copy if on_vector else nc.scalar.copy
             copy(y[n][:, :M], acc_y[n][:])
 
-        def fetch(u):
-            n, half = divmod(u, 2)
-            back = ring.tile([P, BANK], F32, name="back", bufs=6)
-            nc.vector.tensor_copy(back[:], y[n][:].indirect(pos3_sb[:, 32 * half : 32 * (half + 1)]))
-            return back
+        out_rows = out.rearrange("(b p t) j -> b t p j", p=P, t=PACK)
+        back, damp = {}, {}
 
-        def square(back):
-            damp = ring.tile([P, BANK], F32, name="damp", bufs=6)
-            nc.scalar.activation(damp[:], back[:], ACT.Square)
-            return damp
+        def fetch(step):
+            n, half = divmod(step, NHALF)
+            back[step] = work("work_b")
+            entries = pos3_sb[:, BANK // GROUP * half : BANK // GROUP * (half + 1)]
+            nc.vector.tensor_copy(back[step][:], y[n][:].indirect(entries))
 
-        def finish(u, damp):
-            n, half = divmod(u, 2)
+        def square(step):
+            damp[step] = work("work_a")
+            nc.scalar.activation(damp[step][:], back[step][:], ACT.Square)
+
+        def inverse_root(step):
+            nc.scalar.activation(back[step][:], damp[step][:], ACT.Abs_reciprocal_sqrt, bias=one[:])
+
+        def square_again(step):
+            nc.scalar.activation(damp[step][:], back[step][:], ACT.Square)
+
+        def scale_and_store(step):
+            n, half = divmod(step, NHALF)
             b, t = divmod(n, PACK)
-            cols = slice(BANK * half, BANK * (half + 1))
-            res = h[n][:, cols]
-            nc.vector.scalar_tensor_tensor(res, res, gain_sb[:, b, t : t + 1], damp[:], ALU.mult, ALU.mult)
-            nc.sync.dma_start(out_rows[b, t, :, cols], res)
+            probes = slice(BANK * half, BANK * (half + 1))
+            result = h[n][:, probes]
+            nc.vector.scalar_tensor_tensor(result, result, gain_sb[:, b, t : t + 1], damp[step][:], ALU.mult, ALU.mult)
+            nc.sync.dma_start(out_rows[b, t, :, probes], result)
 
-        backs, damps = {}, {}
-        nunit = 2 * ntile
-        kettle_result(0)
-        kettle_result(1)
-        kettle_result(2)
-        for u in range(nunit + 4):
-            if u % 2 == 1 and u // 2 + 3 < ntile:
-                kettle_result(u // 2 + 3)
-            if u < nunit:
-                backs[u] = fetch(u)
-            if 0 <= u - 1 < nunit:
-                damps[u - 1] = square(backs[u - 1])
-            if 0 <= u - 2 < nunit:
-                nc.scalar.activation(backs[u - 2][:], damps[u - 2][:], ACT.Abs_reciprocal_sqrt, bias=1.0)
-            if 0 <= u - 3 < nunit:
-                nc.scalar.activation(damps[u - 3][:], backs[u - 3][:], ACT.Square)
-            if 0 <= u - 4 < nunit:
-                finish(u - 4, damps[u - 4])
+        steps = (fetch, square, inverse_root, square_again, scale_and_store)
+        ahead = 3
+        for n in range(ahead):
+            copy_y(n)
+        for turn in range(NHALF * NTILE + len(steps) - 1):
+            if turn % NHALF == 1 and turn // NHALF + ahead < NTILE:
+                copy_y(turn // NHALF + ahead)
+            for lag, do in enumerate(steps):
+                if 0 <= turn - lag < NHALF * NTILE:
+                    do(turn - lag)

from contextlib import ExitStack

import concourse.mybir as mybir
from concourse.masks import make_identity

K, H, T, S, M = 1024, 1024, 4096, 1024, 512
FLOPS = 2 * (2 * K * H * S) + 2 * H * H * M

F32 = mybir.dt.float32
BF16 = mybir.dt.bfloat16
I32 = mybir.dt.int32
U32 = mybir.dt.uint32
U16 = mybir.dt.uint16
U8 = mybir.dt.uint8
FP8X4 = mybir.dt.float8_e4m3fn_x4
FP4X4 = mybir.dt.float4_e2m1fn_x4
ACT = mybir.ActivationFunctionType
ALU = mybir.AluOpType

P = 128
PACK = 4
PASS = P * PACK
NPASS = K // PASS
NBLK = H // PASS
NTILE = NBLK * PACK
BANK = 512
NHALF = S // BANK
QUADRANT = 32
ROWS = 4
GROUP = 16
LINE = 16
SPARE = 32
DEPTH = 6


def tile_list_kettle_seed_monitor_kernel(
    tc, tab_words, tab_scales, offs, pos1, pos2, pos3, wa, wb_words, wb_scales, w2_words, w2_scales, gain, out
):
    nc = tc.nc
    with ExitStack() as ctx:
        keep = ctx.enter_context(tc.tile_pool(name="keep", bufs=1))
        ring = ctx.enter_context(tc.tile_pool(name="ring", bufs=3))
        psum = ctx.enter_context(tc.psum_pool(name="psum", bufs=8))

        def held(shape, dtype, name):
            return keep.tile(shape, dtype, name=name, align_bytes=64)

        def bank():
            return psum.tile([P, BANK], F32, name="bank")

        def work(tag):
            return ring.tile([P, BANK], F32, name=tag, bufs=DEPTH)

        offs_sb = keep.tile([P, S // GROUP], U16, name="offs_sb")
        pos1_sb = keep.tile([P, M // GROUP], U16, name="pos1_sb")
        pos2_sb = keep.tile([P, M // GROUP], U16, name="pos2_sb")
        pos3_sb = keep.tile([P, S // GROUP], U16, name="pos3_sb")
        tab_w = [held([P, T], I32, "tab_w%d" % a) for a in range(NPASS)]
        tab_s = held([P, T], U8, "tab_s")
        v_w = [held([P, S], U32, "v_w%d" % a) for a in range(NPASS)]
        v_s = held([P, S], U8, "v_s")
        wa_raw = [[held([P, PACK, PASS], F32, "wa_raw%d%d" % (b, a)) for a in range(NPASS)] for b in range(NBLK)]
        wa_w = [[held([P, PASS], U32, "wa_w%d%d" % (b, a)) for a in range(NPASS)] for b in range(NBLK)]
        wa_s = [[held([P, PASS], U8, "wa_s%d%d" % (b, a)) for a in range(NPASS)] for b in range(NBLK)]
        wb_w_raw = [held([P, NPASS * PASS], I32, "wb_w_raw%d" % b) for b in range(NBLK)]
        wb_w = [held([P, NPASS * PASS], I32, "wb_w%d" % b) for b in range(NBLK)]
        wb_s_raw = held([P, H], U8, "wb_s_raw")
        wb_s = held([P, H], U8, "wb_s")
        w2_w_raw = held([P, NBLK * H * 2], U8, "w2_w_raw")
        w2_w = held([P, NBLK * H * 2], U8, "w2_w")
        w2_s_raw = held([P, H], U8, "w2_s_raw")
        w2_s = [held([P, H], U8, "w2_s%d" % b) for b in range(NBLK)]
        gain_sb = held([P, NBLK, PACK], F32, "gain_sb")
        h = [held([P, S], F32, "h%d" % n) for n in range(NTILE)]
        picked1 = held([P, PACK, M], F32, "picked1")
        picked2 = held([P, PACK, M], F32, "picked2")
        x_w = [held([P, M], U32, "x_w%d" % b) for b in range(NBLK)]
        x_s = [held([P, M], U8, "x_s%d" % b) for b in range(NBLK)]
        y = [held([P, M + SPARE], F32, "y%d" % n) for n in range(NTILE)]
        seed = held([P, 1], F32, "seed")
        root = held([P, 1], F32, "root")
        one = held([P, 1], F32, "one")
        ident = held([P, P], F32, "ident")
        make_identity(nc, ident[:])

        for plane in (tab_s, wb_s_raw, w2_s_raw, w2_s[1]):
            nc.vector.memset(plane[:].bitcast(I32), 0)
        nc.vector.memset(seed[:], 1.0)
        nc.scalar.activation(root[:], seed[:], ACT.Abs_reciprocal_sqrt)
        nc.scalar.activation(one[:], root[:], ACT.Sign)
        for n in range(NTILE):
            nc.vector.memset(y[n][:, M:], 0.0)

        def load_tab_words(a):
            nc.sync.dma_start(tab_w[a][:], tab_words[a].rearrange("p t i -> p (t i)").bitcast(I32))

        def load_planes(tile, scales):
            for q in range(P // QUADRANT):
                nc.sync.dma_start(
                    tile[QUADRANT * q : QUADRANT * q + 2 * ROWS, :].bitcast(I32),
                    scales[:, ROWS * q : ROWS * (q + 1), :].bitcast(I32),
                )

        def load_wa(b, a):
            part = wa[PASS * a : PASS * (a + 1), PASS * b : PASS * (b + 1)]
            nc.sync.dma_start(wa_raw[b][a][:], part.rearrange("(p j) c -> p j c", j=PACK))

        def load_wb_words(b):
            part = wb_words[:, :, PASS * b : PASS * (b + 1), :].rearrange("a p c i -> p a (c i)")
            nc.sync.dma_start(wb_w_raw[b][:].rearrange("p (a c) -> p a c", a=NPASS), part.bitcast(I32))

        load_tab_words(0)
        load_planes(tab_s, tab_scales)
        nc.sync.dma_start(offs_sb[:], offs)
        load_tab_words(1)
        load_wb_words(0)
        load_planes(wb_s_raw, wb_scales)
        nc.sync.dma_start(
            w2_w_raw[:].bitcast(I32).rearrange("p (b c) -> p b c", b=NBLK),
            w2_words.rearrange("b p c -> p b c").bitcast(I32),
        )
        load_wa(0, 0)
        load_wa(0, 1)
        nc.sync.dma_start(pos1_sb[:], pos1)
        nc.sync.dma_start(pos2_sb[:], pos2)
        load_planes(w2_s_raw, w2_scales)
        load_wa(1, 0)
        load_wa(1, 1)
        load_wb_words(1)
        nc.sync.dma_start(pos3_sb[:], pos3)
        nc.sync.dma_start(gain_sb[:], gain.rearrange("(b p t) -> p b t", p=P, t=PACK))

        def deal(dst, src, element_bytes):
            run = LINE // element_bytes
            nc.vector.tensor_copy(
                dst.rearrange("p (g t c i) -> p g c t i", t=PACK, c=P // run, i=run),
                src.rearrange("p (g c i t) -> p g c t i", t=PACK, c=P // run, i=run),
            )

        def quantise_wa(b, a, t_first, t_count, copy):
            wa_bf = ring.tile([P, P * t_count * PACK], BF16, name="wa_bf", align_bytes=64)
            copy(
                wa_bf[:].rearrange("p (t m j) -> p m t j", t=t_count, j=PACK),
                wa_raw[b][a][:].rearrange("p j (m t) -> p m t j", t=PACK)[:, :, t_first : t_first + t_count, :],
            )
            cols = slice(P * t_first, P * (t_first + t_count))
            nc.vector.quantize_mx(out=wa_w[b][a][:, cols].bitcast(FP8X4), scales=wa_s[b][a][:, cols], in_=wa_bf[:])

        nc.vector.tensor_copy(v_w[0][:], tab_w[0][:].bitcast(U32).indirect(offs_sb[:]))
        nc.vector.tensor_copy(v_s[:], tab_s[:].indirect(offs_sb[:]))
        nc.vector.tensor_copy(v_w[1][:], tab_w[1][:].bitcast(U32).indirect(offs_sb[:]))
        deal(wb_s[:], wb_s_raw[:], 1)
        deal(wb_w[0][:], wb_w_raw[0][:], 4)
        deal(w2_w[:].bitcast(U16), w2_w_raw[:].bitcast(U16), 2)
        quantise_wa(0, 0, 0, PACK, nc.scalar.copy)
        quantise_wa(0, 1, 0, PACK // 2, nc.vector.tensor_copy)
        quantise_wa(0, 1, PACK // 2, PACK // 2, nc.scalar.copy)

        def v_operand(a, probes):
            return v_w[a][:, probes].bitcast(FP8X4), v_s[ROWS * a :, probes]

        def wa_operand(a, n):
            b, t = divmod(n, PACK)
            cols = slice(P * t, P * (t + 1))
            return wa_w[b][a][:, cols].bitcast(FP8X4), wa_s[b][a][:, cols]

        def wb_operand(a, n):
            b, t = divmod(n, PACK)
            words = wb_w[b][:, PASS * a + P * t : PASS * a + P * (t + 1)]
            return words.bitcast(FP8X4), wb_s[ROWS * a :, P * n : P * (n + 1)]

        def mx_pass(acc, stationary, moving, a, passes):
            nc.tensor.matmul_mx(
                out=acc,
                lhsT=stationary[0],
                lhsT_scale=stationary[1],
                rhs=moving[0],
                rhs_scale=moving[1],
                start=(a == 0),
                stop=(a == passes - 1),
            )

        def direct_half(n, half):
            probes = slice(BANK * half, BANK * (half + 1))
            acc_b = bank()
            for a in range(NPASS):
                mx_pass(acc_b[:], wb_operand(a, n), v_operand(a, probes), a, NPASS)
            acc_a = bank()
            for a in range(NPASS):
                mx_pass(acc_a[:], wa_operand(a, n), v_operand(a, probes), a, NPASS)
            size = work("work_a")
            nc.scalar.activation(size[:], acc_b[:], ACT.Abs)
            nc.vector.tensor_tensor(h[n][:, probes], acc_a[:], size[:], ALU.subtract)

        def turned_terms(n, half):
            acc_b = bank()
            acc_a = bank()
            for acc, weight in ((acc_b, wb_operand), (acc_a, wa_operand)):
                for piece in range(BANK // P):
                    probes = slice(BANK * half + P * piece, BANK * half + P * (piece + 1))
                    for a in range(NPASS):
                        mx_pass(acc[:, P * piece : P * (piece + 1)], v_operand(a, probes), weight(a, n), a, NPASS)
            size = work("work_a")
            nc.scalar.activation(size[:], acc_b[:], ACT.Abs)
            minus_a = work("work_b")
            nc.scalar.activation(minus_a[:], acc_a[:], ACT.Copy, scale=-1.0)
            return size, minus_a

        def turn_back(n, half, size, minus_a):
            acc_h = bank()
            for piece in range(BANK // P):
                cols = slice(P * piece, P * (piece + 1))
                nc.tensor.matmul(acc_h[:, cols], size[:, cols], ident[:], start=True, stop=False, is_transpose=True)
                nc.tensor.matmul(acc_h[:, cols], minus_a[:, cols], ident[:], start=False, stop=True, is_transpose=True)
            nc.scalar.activation(h[n][:, BANK * half : BANK * (half + 1)], acc_h[:], ACT.Copy, scale=-1.0)

        def is_turned(n, half):
            return (half == 1 and n > 0) or (n >= 3 and n % 2 == 1)

        terms = {}

        def make_half(step):
            if step < NHALF * NTILE:
                n, half = divmod(step, NHALF)
                if is_turned(n, half):
                    terms[step] = turned_terms(n, half)
                else:
                    direct_half(n, half)
            if step - 1 in terms:
                turn_back(*divmod(step - 1, NHALF), *terms[step - 1])

        def pick(n, picked, pos_sb):
            nc.vector.tensor_copy(picked[:, n % PACK, :], h[n][:].indirect(pos_sb[:]))

        def quantise_x(b):
            kettles = [slice(M // 2 * side, M // 2 * (side + 1)) for side in range(2)]
            x_bf = [ring.tile([P, M // 2 * PACK], BF16, name="x_bf", align_bytes=64, bufs=2) for side in range(2)]
            for side in range(2):
                nc.vector.tensor_tensor(
                    x_bf[side][:].rearrange("p (c i t) -> p c t i", i=2, t=PACK),
                    picked1[:, :, kettles[side]].rearrange("p t (c i) -> p c t i", i=2),
                    picked2[:, :, kettles[side]].rearrange("p t (c i) -> p c t i", i=2),
                    ALU.max,
                )
            for side in range(2):
                nc.vector.quantize_mx(
                    out=x_w[b][:, kettles[side]].bitcast(FP8X4), scales=x_s[b][:, kettles[side]], in_=x_bf[side][:]
                )

        def deal_w2_planes():
            deal(w2_s[0][:], w2_s_raw[:], 1)
            for q in range(P // QUADRANT):
                first = QUADRANT * q
                nc.sync.dma_start(
                    w2_s[1][first : first + ROWS, :].bitcast(I32),
                    w2_s[0][first + ROWS : first + 2 * ROWS, :].bitcast(I32),
                )

        for n in range(NTILE + 1):
            make_half(NHALF * n)
            if n > 0:
                pick(n - 1, picked1, pos1_sb)
            if n < NTILE:
                make_half(NHALF * n + 1)
            if n > 0:
                pick(n - 1, picked2, pos2_sb)
                if n % PACK == 0:
                    quantise_x(n // PACK - 1)
            if n == 0:
                deal_w2_planes()
            if n == 1:
                quantise_wa(1, 0, 0, PACK, nc.scalar.copy)
            if n == 2:
                quantise_wa(1, 1, 0, PACK, nc.scalar.copy)
                deal(wb_w[1][:], wb_w_raw[1][:], 4)

        acc_y = [bank() for n in range(NTILE)]
        for b in range(NBLK):
            for n in range(NTILE):
                first = H * b + P * n
                w2_operand = w2_w[:, 2 * first : 2 * (first + P)].bitcast(FP4X4), w2_s[b][:, P * n : P * (n + 1)]
                mx_pass(acc_y[n][:], w2_operand, (x_w[b][:].bitcast(FP8X4), x_s[b][:]), b, NBLK)

        def copy_y(n):
            on_vector = n == 0 or (n >= PACK and n % 2 == 0)
            copy = nc.vector.tensor_copy if on_vector else nc.scalar.copy
            copy(y[n][:, :M], acc_y[n][:])

        out_rows = out.rearrange("(b p t) j -> b t p j", p=P, t=PACK)
        back, damp = {}, {}

        def fetch(step):
            n, half = divmod(step, NHALF)
            back[step] = work("work_b")
            entries = pos3_sb[:, BANK // GROUP * half : BANK // GROUP * (half + 1)]
            nc.vector.tensor_copy(back[step][:], y[n][:].indirect(entries))

        def square(step):
            damp[step] = work("work_a")
            nc.scalar.activation(damp[step][:], back[step][:], ACT.Square)

        def inverse_root(step):
            nc.scalar.activation(back[step][:], damp[step][:], ACT.Abs_reciprocal_sqrt, bias=one[:])

        def square_again(step):
            nc.scalar.activation(damp[step][:], back[step][:], ACT.Square)

        def scale_and_store(step):
            n, half = divmod(step, NHALF)
            b, t = divmod(n, PACK)
            probes = slice(BANK * half, BANK * (half + 1))
            result = h[n][:, probes]
            nc.vector.scalar_tensor_tensor(result, result, gain_sb[:, b, t : t + 1], damp[step][:], ALU.mult, ALU.mult)
            nc.sync.dma_start(out_rows[b, t, :, probes], result)

        steps = (fetch, square, inverse_root, square_again, scale_and_store)
        ahead = 3
        for n in range(ahead):
            copy_y(n)
        for turn in range(NHALF * NTILE + len(steps) - 1):
            if turn % NHALF == 1 and turn // NHALF + ahead < NTILE:
                copy_y(turn // NHALF + ahead)
            for lag, do in enumerate(steps):
                if 0 <= turn - lag < NHALF * NTILE:
                    do(turn - lag)
